import numpy as np
import ml_dtypes


def mxq(x, axis, fmt="e4m3"):
    dtype, down = {"e4m3": (ml_dtypes.float8_e4m3fn, 7), "e5m2": (ml_dtypes.float8_e5m2, 14)}[fmt]
    v = np.moveaxis(np.asarray(x, np.float32).astype(ml_dtypes.bfloat16).astype(np.float64), axis, -1)
    blocks = v.reshape(v.shape[:-1] + (-1, 32))
    amax = np.abs(blocks).max(-1, keepdims=True)
    byte = np.maximum(np.where(amax > 0, np.frexp(amax)[1] - 1 + 127, 0) - down, 1)
    scale = np.exp2(byte - 127.0)
    codes = (blocks / scale).astype(np.float32).astype(dtype).astype(np.float64)
    return np.moveaxis((codes * scale).reshape(v.shape), -1, axis)


WIDE = False


def mx_kscale(k, group=512):
    if not WIDE:
        return np.ones(k)
    levels = np.array([10, -10, 5, -5, 0])
    if group != 512:
        return np.exp2(np.random.permutation(np.resize(levels, k // group))).repeat(group)
    if k % 512:
        return np.exp2(np.random.permutation(np.resize(levels, k // 32))).repeat(32)
    a = np.empty((k // 512, 16))
    for p in range(k // 512):
        a[p, :8] = np.random.permutation(np.resize(levels, 8))
        for g in range(8):
            far = levels[np.abs(levels - a[p, g]) >= 10]
            a[p, g + 8] = far[np.random.randint(len(far))]
    return np.exp2(a.ravel()).repeat(32)


def f64(x):
    return np.asarray(x).astype(np.float64)


E2M1 = np.array([0.0, 0.5, 1.0, 1.5, 2.0, 3.0, 4.0, 6.0, -0.0, -0.5, -1.0, -1.5, -2.0, -3.0, -4.0, -6.0])


def pack_group(w):
    k, n = w.shape
    w = f64(np.asarray(w, np.float32).astype(ml_dtypes.bfloat16)).reshape(k // 32, 32, n)
    amax = np.abs(w).max(1)
    mant, ex = np.frexp(amax / 6.0)
    byte = np.clip(np.where(amax > 0, np.where(mant > 0.5, ex, ex - 1) + 127, 1), 1, 254)
    scaled = (w * np.exp2(127.0 - byte)[:, None, :]).reshape(k, n).astype(np.float32)
    c = np.ascontiguousarray(scaled.reshape(k // 4, 4, n).transpose(0, 2, 1)).astype(ml_dtypes.float4_e2m1fn).view(np.uint8) & 0xF
    return np.ascontiguousarray((c[..., 0::2] | (c[..., 1::2] << 4)).reshape(k // 4, 2 * n)), byte.astype(np.uint8)


def unpack_group(words, scales):
    p, n = words.shape[0], scales.shape[1]
    words = np.ascontiguousarray(words).reshape(p, n, 2)
    nib = np.empty((p, n, 4), np.uint8)
    nib[..., 0::2] = words & 0xF
    nib[..., 1::2] = words >> 4
    return E2M1[nib].transpose(0, 2, 1).reshape(4 * p, n) * np.repeat(np.exp2(scales.astype(np.float64) - 127.0), 32, axis=0)


def sigmoid(v):
    return 1.0 / (1.0 + np.exp(-v))


G, D, M, O, N = 2, 256, 256, 256, 512


def setup_inputs():
    n = np.random.standard_normal
    s_d = mx_kscale(D, 0)
    s_o = mx_kscale(O, 0)
    w1_ = [pack_group(w) for w in n((G, D, M)) / np.sqrt(D) / s_d[:, None]]
    w2_ = [pack_group(w) for w in n((G, D, M)) / np.sqrt(D) / s_d[:, None]]
    wo_ = [pack_group(w) for w in n((G, O, M)) / np.sqrt(O) / s_o[:, None]]
    return {
        "x": (n((G, D, N)) * s_d[:, None]).astype(np.float32),
        "w1_words": np.stack([w[0] for w in w1_]),
        "w1_scales": np.stack([w[1] for w in w1_]),
        "w2_words": np.stack([w[0] for w in w2_]),
        "w2_scales": np.stack([w[1] for w in w2_]),
        "gn": (np.random.uniform(0.5, 2.0, (G, M, 1))).astype(np.float32),
        "wo_words": np.stack([w[0] for w in wo_]),
        "wo_scales": np.stack([w[1] for w in wo_]),
        "dy": (n((G, O, N)) * s_o[:, None]).astype(np.float32),
        "old": (0.3 * n((G, M, N))).astype(np.float32),
    }


def reference(x, w1_words, w1_scales, w2_words, w2_scales, gn, wo_words, wo_scales, dy, old):
    w1 = np.stack([unpack_group(w1_words[g], w1_scales[g]) for g in range(G)])
    xq = mxq(f64(x), 1, "e4m3")
    z1 = w1.transpose(0, 2, 1) @ xq
    w2 = np.stack([unpack_group(w2_words[g], w2_scales[g]) for g in range(G)])
    z2 = w2.transpose(0, 2, 1) @ xq
    rm = np.sqrt(np.mean(np.square(z1), axis=-1, keepdims=True) + 0.01)
    wo = np.stack([unpack_group(wo_words[g], wo_scales[g]) for g in range(G)])
    dyq = mxq(f64(dy), 1, "e4m3")
    c0 = wo.transpose(0, 2, 1) @ dyq
    dnz = c0 * sigmoid(z2)
    drm = np.sum(dnz * f64(gn) * z1 / np.square(rm) * (-1.0), axis=-1, keepdims=True)
    dz1 = dnz * f64(gn) / rm + drm * 0.5 / np.sqrt(np.mean(np.square(z1), axis=-1, keepdims=True) + 0.01) / 512.0 * z1 * 2.0
    y = dz1 + f64(old)
    return y

@@ -1,0 +1,227 @@
+import math
+from contextlib import ExitStack
+
+import concourse.mybir as mybir
+
+G, D, M, N = 2, 256, 256, 512
+FLOPS = 3 * 2 * G * D * M * N
+EPS = 0.01
+
+F32 = mybir.dt.float32
+BF16 = mybir.dt.bfloat16
+I32 = mybir.dt.int32
+U32 = mybir.dt.uint32
+U8 = mybir.dt.uint8
+FP8X4 = mybir.dt.float8_e4m3fn_x4
+FP4X4 = mybir.dt.float4_e2m1fn_x4
+ALU = mybir.AluOpType
+ACT = mybir.ActivationFunctionType
+
+P = 128
+PACK = 4
+ROWS = D // PACK
+QUAD = 32
+HALVES = M // P
+HALF_N = N // 2
+X_VECTOR_COLS = 64
+
+
+def tile_rows_brownorm_kernel(tc, x, w1_words, w1_scales, w2_words, w2_scales, gn, wo_words, wo_scales, dy, old, out):
+    nc = tc.nc
+    with ExitStack() as ctx:
+        sb = ctx.enter_context(tc.tile_pool(name="sb", bufs=1))
+        ps = ctx.enter_context(tc.psum_pool(name="ps", bufs=1))
+        ctx.enter_context(tc.manual_schedule())
+
+        def new(name, shape, dtype):
+            return sb.tile(shape, dtype, name=name, align_bytes=64)
+
+        def load_rows(name, src):
+            raw = new(name, [P, PACK, N], F32)
+            nc.sync.dma_start(out=raw[:], in_=src.rearrange("g (p j) n -> (g p) j n", j=PACK))
+            return raw
+
+        def load_words(name, src):
+            words = new(name, [P, 2 * M], U8)
+            nc.sync.dma_start(out=words[:].bitcast(I32), in_=src.rearrange("g p b -> (g p) b").bitcast(I32))
+            return words
+
+        def zeroed_plane(name):
+            plane = new(name, [P, M], U8)
+            nc.vector.memset(plane[:].bitcast(I32), 0)
+            return plane
+
+        def load_scales(queue, plane, src):
+            rows = src.rearrange("g t m -> (g t) m").bitcast(I32)
+            for q in range(P // QUAD):
+                queue.dma_start(out=plane[QUAD * q : QUAD * q + 4, :].bitcast(I32), in_=rows[4 * q : 4 * q + 4, :])
+
+        def interleave(copy, dst, raw, half, lo, hi):
+            cols = slice(half * HALF_N + lo, half * HALF_N + hi)
+            copy(
+                out=dst[:, lo:hi, :].rearrange("p (c i) j -> p c j i", i=4),
+                in_=raw[:, :, cols].rearrange("p j (c i) -> p c j i", i=4),
+            )
+
+        def quantize(codes, scales, grouped, half):
+            cols = slice(half * HALF_N, (half + 1) * HALF_N)
+            nc.vector.quantize_mx(
+                out=codes[:, cols].bitcast(FP8X4), scales=scales[:, cols], in_=grouped[:].rearrange("p c j -> p (c j)")
+            )
+
+        def product(bank, words, plane, codes, scales, g, h):
+            rows = slice(ROWS * g, ROWS * (g + 1))
+            nc.tensor.matmul_mx(
+                out=bank[:],
+                lhsT=words[rows, 2 * P * h : 2 * P * (h + 1)].bitcast(FP4X4),
+                lhsT_scale=plane[rows, P * h : P * (h + 1)],
+                rhs=codes[rows, :].bitcast(FP8X4),
+                rhs_scale=scales[rows, :],
+                start=True,
+                stop=True,
+            )
+
+        w1_plane = zeroed_plane("w1_plane")
+        gain_rows = new("gain_rows", [P, P], F32)
+        nc.vector.memset(gain_rows[:], 0.0)
+        w2_plane = zeroed_plane("w2_plane")
+        wo_plane = zeroed_plane("wo_plane")
+        minus_half = new("minus_half", [P, G], F32)
+        nc.vector.memset(minus_half[:], -0.5)
+
+        x_raw = load_rows("x_raw", x)
+        load_scales(nc.sync, w1_plane, w1_scales)
+        w1 = load_words("w1", w1_words)
+        w2 = load_words("w2", w2_words)
+        dy_raw = load_rows("dy_raw", dy)
+        load_scales(nc.sync, wo_plane, wo_scales)
+        wo = load_words("wo", wo_words)
+        old_sb = new("old_sb", [P, G * HALVES, N], F32)
+        nc.sync.dma_start(out=old_sb[:], in_=old.rearrange("g (h p) n -> p (g h) n", p=P))
+
+        nc.gpsimd.dma_start(
+            out=gain_rows[0:P:QUAD, :].rearrange("q (c i) -> q c i", i=QUAD),
+            in_=gn.rearrange("g m o -> (g m o)").rearrange("(c q i) -> q c i", q=P // QUAD, i=QUAD),
+        )
+        load_scales(nc.gpsimd, w2_plane, w2_scales)
+
+        x_codes, x_scales = new("x_codes", [P, N], U32), new("x_scales", [P, N], U8)
+        x_lo, x_hi = new("x_lo", [P, HALF_N, PACK], BF16), new("x_hi", [P, HALF_N, PACK], BF16)
+        interleave(nc.vector.tensor_copy, x_lo, x_raw, 0, 0, HALF_N)
+        interleave(nc.scalar.copy, x_hi, x_raw, 1, X_VECTOR_COLS, HALF_N)
+        interleave(nc.vector.tensor_copy, x_hi, x_raw, 1, 0, X_VECTOR_COLS)
+        quantize(x_codes, x_scales, x_lo, 0)
+        quantize(x_codes, x_scales, x_hi, 1)
+
+        z1 = {(g, h): ps.tile([P, N], F32, name="z1_%d_%d" % (g, h)) for g in range(G) for h in range(HALVES)}
+        z2 = [ps.tile([P, N], F32, name="z2_%d" % g) for g in range(G)]
+        c0 = [ps.tile([P, N], F32, name="c0_%d" % g) for g in range(G)]
+
+        def z1_products(h):
+            for g in range(G):
+                product(z1[g, h], w1, w1_plane, x_codes, x_scales, g, h)
+
+        def z2_products(h):
+            for g in range(G):
+                product(z2[g], w2, w2_plane, x_codes, x_scales, g, h)
+
+        product(z2[0], w2, w2_plane, x_codes, x_scales, 0, 0)
+        product(z1[1, 0], w1, w1_plane, x_codes, x_scales, 1, 0)
+        product(z1[0, 0], w1, w1_plane, x_codes, x_scales, 0, 0)
+        product(z2[1], w2, w2_plane, x_codes, x_scales, 1, 0)
+        z1_products(1)
+
+        gain_cols = new("gain_cols", [P, P], F32)
+        nc.vector.transpose(gain_cols[:], gain_rows[:])
+        factors = new("factors", [P, 2, 8], F32)
+        nc.vector.tensor_scalar(
+            factors[:, 0, 0 : HALVES * G].rearrange("p (h g) -> p h g", g=G),
+            gain_cols[:].rearrange("p (g h i) -> p h g i", g=G, h=HALVES)[:, :, :, 0],
+            -math.sqrt(N),
+            None,
+            ALU.mult,
+        )
+
+        dy_codes, dy_scales = new("dy_codes", [P, N], U32), new("dy_scales", [P, N], U8)
+        dy_halves = [new("dy_half%d" % half, [P, HALF_N, PACK], BF16) for half in range(2)]
+        for half in range(2):
+            interleave(nc.vector.tensor_copy, dy_halves[half], dy_raw, half, 0, HALF_N)
+        for half in range(2):
+            quantize(dy_codes, dy_scales, dy_halves[half], half)
+
+        def c0_products(h):
+            for g in range(G):
+                product(c0[g], wo, wo_plane, dy_codes, dy_scales, g, h)
+
+        square_sums, coefs, gate, grad, slope, summed = {}, {}, {}, {}, {}, {}
+
+        for h in range(HALVES):
+            square_sums[h] = new("square_sums%d" % h, [P, G], F32)
+
+        def sum_squares(g, h):
+            squares = new("squares_%d_%d" % (g, h), [P, N], BF16)
+            nc.scalar.activation(squares[:], z1[g, h][:], ACT.Square, accum_out=square_sums[h][:, g : g + 1])
+
+        def row_coefs(h):
+            total = new("total%d" % h, [P, G], F32)
+            nc.gpsimd.tensor_scalar(total[:], square_sums[h][:], N * EPS, 1.0, ALU.add, ALU.mult)
+            cols = slice(G * h, G * (h + 1))
+            nc.gpsimd.tensor_tensor(factors[:, 1, cols], total[:], minus_half[:], ALU.pow)
+            coefs[h] = new("coefs%d" % h, [P, 2, G], F32)
+            nc.gpsimd.tensor_tensor(coefs[h][:], factors[:, :, cols], factors[:, 1:2, cols].to_broadcast([P, 2, G]), ALU.mult)
+
+        def make_gate(g, h):
+            gate[g, h] = new("gate_%d_%d" % (g, h), [P, N], F32)
+            nc.scalar.activation(gate[g, h][:], z2[g][:], ACT.Sigmoid)
+
+        def first_term(g, h):
+            grad[g, h] = new("grad_%d_%d" % (g, h), [P, N], F32)
+            nc.vector.scalar_tensor_tensor(
+                grad[g, h][:], c0[g][:], coefs[h][:, 0, g : g + 1], gate[g, h][:], ALU.mult, ALU.mult
+            )
+
+        def add_old(g, h):
+            summed[g, h] = new("summed_%d_%d" % (g, h), [P, N], F32)
+            nc.gpsimd.tensor_tensor(summed[g, h][:], old_sb[:, HALVES * g + h, :], grad[g, h][:], ALU.subtract)
+
+        def row_slope(g, h):
+            terms = new("terms_%d_%d" % (g, h), [P, N], F32)
+            slope[g, h] = new("slope_%d_%d" % (g, h), [P, 1], F32)
+            nc.vector.scalar_tensor_tensor(
+                terms[:], z1[g, h][:], coefs[h][:, 1, g : g + 1], grad[g, h][:], ALU.mult, ALU.mult, accum_out=slope[g, h][:]
+            )
+
+        def finish(g, h):
+            result = new("result_%d_%d" % (g, h), [P, N], F32)
+            nc.vector.scalar_tensor_tensor(result[:], z1[g, h][:], slope[g, h][:], summed[g, h][:], ALU.mult, ALU.add)
+            nc.sync.dma_start(out=out[g, P * h : P * (h + 1), :], in_=result[:])
+
+        make_gate(0, 0)
+        sum_squares(1, 0)
+        sum_squares(0, 0)
+        make_gate(1, 0)
+        row_coefs(0)
+        c0_products(0)
+        z2_products(1)
+        sum_squares(0, 1)
+        sum_squares(1, 1)
+        make_gate(0, 1)
+        make_gate(1, 1)
+        first_term(0, 0)
+        add_old(0, 0)
+        row_coefs(1)
+        first_term(1, 0)
+        add_old(1, 0)
+        c0_products(1)
+        row_slope(0, 0)
+        row_slope(1, 0)
+        finish(0, 0)
+        first_term(0, 1)
+        add_old(0, 1)
+        finish(1, 0)
+        first_term(1, 1)
+        add_old(1, 1)
+        row_slope(0, 1)
+        row_slope(1, 1)
+        finish(0, 1)
+        finish(1, 1)

@@ -82,28 +82,30 @@ def tile_rows_brownorm_kernel(tc, x, w1_words, w1_scales, w2_words, w2_scales, g
             )
 
         w1_plane = zeroed_plane("w1_plane")
+        wo_plane = zeroed_plane("wo_plane")
         gain_rows = new("gain_rows", [P, P], F32)
         nc.vector.memset(gain_rows[:], 0.0)
         w2_plane = zeroed_plane("w2_plane")
-        wo_plane = zeroed_plane("wo_plane")
         minus_half = new("minus_half", [P, G], F32)
         nc.vector.memset(minus_half[:], -0.5)
+        warm = new("warm", [P, G], F32)
+        nc.scalar.activation(warm[:], minus_half[:], ACT.Sigmoid)
 
         x_raw = load_rows("x_raw", x)
         load_scales(nc.sync, w1_plane, w1_scales)
         w1 = load_words("w1", w1_words)
-        w2 = load_words("w2", w2_words)
+        nc.sync.dma_start(
+            out=gain_rows[0:P:QUAD, :].rearrange("q (c i) -> q c i", i=QUAD),
+            in_=gn.rearrange("g m o -> (g m o)").rearrange("(c q i) -> q c i", q=P // QUAD, i=QUAD),
+        )
         dy_raw = load_rows("dy_raw", dy)
-        load_scales(nc.sync, wo_plane, wo_scales)
+        load_scales(nc.sync, w2_plane, w2_scales)
+        w2 = load_words("w2", w2_words)
         wo = load_words("wo", wo_words)
         old_sb = new("old_sb", [P, G * HALVES, N], F32)
         nc.sync.dma_start(out=old_sb[:], in_=old.rearrange("g (h p) n -> p (g h) n", p=P))
 
-        nc.gpsimd.dma_start(
-            out=gain_rows[0:P:QUAD, :].rearrange("q (c i) -> q c i", i=QUAD),
-            in_=gn.rearrange("g m o -> (g m o)").rearrange("(c q i) -> q c i", q=P // QUAD, i=QUAD),
-        )
-        load_scales(nc.gpsimd, w2_plane, w2_scales)
+        load_scales(nc.gpsimd, wo_plane, wo_scales)
 
         x_codes, x_scales = new("x_codes", [P, N], U32), new("x_scales", [P, N], U8)
         x_lo, x_hi = new("x_lo", [P, HALF_N, PACK], BF16), new("x_hi", [P, HALF_N, PACK], BF16)
@@ -117,19 +119,17 @@ def tile_rows_brownorm_kernel(tc, x, w1_words, w1_scales, w2_words, w2_scales, g
         z2 = [ps.tile([P, N], F32, name="z2_%d" % g) for g in range(G)]
         c0 = [ps.tile([P, N], F32, name="c0_%d" % g) for g in range(G)]
 
-        def z1_products(h):
-            for g in range(G):
-                product(z1[g, h], w1, w1_plane, x_codes, x_scales, g, h)
+        def z1_product(g, h):
+            product(z1[g, h], w1, w1_plane, x_codes, x_scales, g, h)
 
-        def z2_products(h):
-            for g in range(G):
-                product(z2[g], w2, w2_plane, x_codes, x_scales, g, h)
+        def z2_product(g, h):
+            product(z2[g], w2, w2_plane, x_codes, x_scales, g, h)
 
-        product(z2[0], w2, w2_plane, x_codes, x_scales, 0, 0)
-        product(z1[1, 0], w1, w1_plane, x_codes, x_scales, 1, 0)
-        product(z1[0, 0], w1, w1_plane, x_codes, x_scales, 0, 0)
-        product(z2[1], w2, w2_plane, x_codes, x_scales, 1, 0)
-        z1_products(1)
+        z1_product(0, 0)
+        z1_product(1, 0)
+        z2_product(0, 0)
+        z2_product(1, 0)
+        z1_product(0, 1)
 
         gain_cols = new("gain_cols", [P, P], F32)
         nc.vector.transpose(gain_cols[:], gain_rows[:])
@@ -149,9 +149,8 @@ def tile_rows_brownorm_kernel(tc, x, w1_words, w1_scales, w2_words, w2_scales, g
         for half in range(2):
             quantize(dy_codes, dy_scales, dy_halves[half], half)
 
-        def c0_products(h):
-            for g in range(G):
-                product(c0[g], wo, wo_plane, dy_codes, dy_scales, g, h)
+        def c0_product(g, h):
+            product(c0[g], wo, wo_plane, dy_codes, dy_scales, g, h)
 
         square_sums, coefs, gate, grad, slope, summed = {}, {}, {}, {}, {}, {}
 
@@ -162,13 +161,15 @@ def tile_rows_brownorm_kernel(tc, x, w1_words, w1_scales, w2_words, w2_scales, g
             squares = new("squares_%d_%d" % (g, h), [P, N], BF16)
             nc.scalar.activation(squares[:], z1[g, h][:], ACT.Square, accum_out=square_sums[h][:, g : g + 1])
 
-        def row_coefs(h):
+        def inverse_roots(h):
             total = new("total%d" % h, [P, G], F32)
-            nc.gpsimd.tensor_scalar(total[:], square_sums[h][:], N * EPS, 1.0, ALU.add, ALU.mult)
-            cols = slice(G * h, G * (h + 1))
-            nc.gpsimd.tensor_tensor(factors[:, 1, cols], total[:], minus_half[:], ALU.pow)
-            coefs[h] = new("coefs%d" % h, [P, 2, G], F32)
-            nc.gpsimd.tensor_tensor(coefs[h][:], factors[:, :, cols], factors[:, 1:2, cols].to_broadcast([P, 2, G]), ALU.mult)
+            nc.scalar.activation(total[:], square_sums[h][:], ACT.Copy, bias=N * EPS)
+            nc.gpsimd.tensor_tensor(factors[:, 1, G * h : G * (h + 1)], total[:], minus_half[:], ALU.pow)
+
+        def row_coefs(g, h):
+            col = G * h + g
+            coefs[g, h] = new("coefs_%d_%d" % (g, h), [P, 2], F32)
+            nc.scalar.activation(coefs[g, h][:], factors[:, :, col], ACT.Copy, scale=factors[:, 1, col : col + 1])
 
         def make_gate(g, h):
             gate[g, h] = new("gate_%d_%d" % (g, h), [P, N], F32)
@@ -177,7 +178,7 @@ def tile_rows_brownorm_kernel(tc, x, w1_words, w1_scales, w2_words, w2_scales, g
         def first_term(g, h):
             grad[g, h] = new("grad_%d_%d" % (g, h), [P, N], F32)
             nc.vector.scalar_tensor_tensor(
-                grad[g, h][:], c0[g][:], coefs[h][:, 0, g : g + 1], gate[g, h][:], ALU.mult, ALU.mult
+                grad[g, h][:], c0[g][:], coefs[g, h][:, 0:1], gate[g, h][:], ALU.mult, ALU.mult
             )
 
         def add_old(g, h):
@@ -188,7 +189,7 @@ def tile_rows_brownorm_kernel(tc, x, w1_words, w1_scales, w2_words, w2_scales, g
             terms = new("terms_%d_%d" % (g, h), [P, N], F32)
             slope[g, h] = new("slope_%d_%d" % (g, h), [P, 1], F32)
             nc.vector.scalar_tensor_tensor(
-                terms[:], z1[g, h][:], coefs[h][:, 1, g : g + 1], grad[g, h][:], ALU.mult, ALU.mult, accum_out=slope[g, h][:]
+                terms[:], z1[g, h][:], coefs[g, h][:, 1:2], grad[g, h][:], ALU.mult, ALU.mult, accum_out=slope[g, h][:]
             )
 
         def finish(g, h):
@@ -196,23 +197,31 @@ def tile_rows_brownorm_kernel(tc, x, w1_words, w1_scales, w2_words, w2_scales, g
             nc.vector.scalar_tensor_tensor(result[:], z1[g, h][:], slope[g, h][:], summed[g, h][:], ALU.mult, ALU.add)
             nc.sync.dma_start(out=out[g, P * h : P * (h + 1), :], in_=result[:])
 
-        make_gate(0, 0)
-        sum_squares(1, 0)
         sum_squares(0, 0)
+        sum_squares(1, 0)
+        make_gate(0, 0)
+        inverse_roots(0)
         make_gate(1, 0)
-        row_coefs(0)
-        c0_products(0)
-        z2_products(1)
-        sum_squares(0, 1)
-        sum_squares(1, 1)
-        make_gate(0, 1)
-        make_gate(1, 1)
+        row_coefs(0, 0)
+        row_coefs(1, 0)
+        c0_product(0, 0)
+        c0_product(1, 0)
+        z1_product(1, 1)
+        z2_product(0, 1)
         first_term(0, 0)
         add_old(0, 0)
-        row_coefs(1)
         first_term(1, 0)
+        c0_product(0, 1)
+        z2_product(1, 1)
+        c0_product(1, 1)
+        sum_squares(0, 1)
+        sum_squares(1, 1)
+        inverse_roots(1)
         add_old(1, 0)
-        c0_products(1)
+        make_gate(0, 1)
+        row_coefs(0, 1)
+        row_coefs(1, 1)
+        make_gate(1, 1)
         row_slope(0, 0)
         row_slope(1, 0)
         finish(0, 0)

@@ -125,11 +125,10 @@ def tile_rows_brownorm_kernel(tc, x, w1_words, w1_scales, w2_words, w2_scales, g
         def z2_product(g, h):
             product(z2[g], w2, w2_plane, x_codes, x_scales, g, h)
 
-        z1_product(0, 0)
-        z1_product(1, 0)
+        for h in range(HALVES):
+            for g in range(G):
+                z1_product(g, h)
         z2_product(0, 0)
-        z2_product(1, 0)
-        z1_product(0, 1)
 
         gain_cols = new("gain_cols", [P, P], F32)
         nc.vector.transpose(gain_cols[:], gain_rows[:])
@@ -166,10 +165,16 @@ def tile_rows_brownorm_kernel(tc, x, w1_words, w1_scales, w2_words, w2_scales, g
             nc.scalar.activation(total[:], square_sums[h][:], ACT.Copy, bias=N * EPS)
             nc.gpsimd.tensor_tensor(factors[:, 1, G * h : G * (h + 1)], total[:], minus_half[:], ALU.pow)
 
-        def row_coefs(g, h):
-            col = G * h + g
-            coefs[g, h] = new("coefs_%d_%d" % (g, h), [P, 2], F32)
-            nc.scalar.activation(coefs[g, h][:], factors[:, :, col], ACT.Copy, scale=factors[:, 1, col : col + 1])
+        def row_coefs_on_vector(h):
+            cols = slice(G * h, G * (h + 1))
+            coefs[h] = new("coefs%d" % h, [P, 2, G], F32)
+            nc.vector.tensor_tensor(coefs[h][:], factors[:, :, cols], factors[:, 1:2, cols].to_broadcast([P, 2, G]), ALU.mult)
+
+        def row_coefs_on_scalar(h):
+            coefs[h] = new("coefs%d" % h, [P, 2, G], F32)
+            for g in range(G):
+                col = G * h + g
+                nc.scalar.activation(coefs[h][:, :, g], factors[:, :, col], ACT.Copy, scale=factors[:, 1, col : col + 1])
 
         def make_gate(g, h):
             gate[g, h] = new("gate_%d_%d" % (g, h), [P, N], F32)
@@ -178,7 +183,7 @@ def tile_rows_brownorm_kernel(tc, x, w1_words, w1_scales, w2_words, w2_scales, g
         def first_term(g, h):
             grad[g, h] = new("grad_%d_%d" % (g, h), [P, N], F32)
             nc.vector.scalar_tensor_tensor(
-                grad[g, h][:], c0[g][:], coefs[g, h][:, 0:1], gate[g, h][:], ALU.mult, ALU.mult
+                grad[g, h][:], c0[g][:], coefs[h][:, 0, g : g + 1], gate[g, h][:], ALU.mult, ALU.mult
             )
 
         def add_old(g, h):
@@ -189,48 +194,51 @@ def tile_rows_brownorm_kernel(tc, x, w1_words, w1_scales, w2_words, w2_scales, g
             terms = new("terms_%d_%d" % (g, h), [P, N], F32)
             slope[g, h] = new("slope_%d_%d" % (g, h), [P, 1], F32)
             nc.vector.scalar_tensor_tensor(
-                terms[:], z1[g, h][:], coefs[g, h][:, 1:2], grad[g, h][:], ALU.mult, ALU.mult, accum_out=slope[g, h][:]
+                terms[:], z1[g, h][:], coefs[h][:, 1, g : g + 1], grad[g, h][:], ALU.mult, ALU.mult, accum_out=slope[g, h][:]
             )
 
-        def finish(g, h):
-            result = new("result_%d_%d" % (g, h), [P, N], F32)
-            nc.vector.scalar_tensor_tensor(result[:], z1[g, h][:], slope[g, h][:], summed[g, h][:], ALU.mult, ALU.add)
-            nc.sync.dma_start(out=out[g, P * h : P * (h + 1), :], in_=result[:])
+        def finish(g, h, pieces=1):
+            width = N // pieces
+            for piece in range(pieces):
+                cols = slice(width * piece, width * (piece + 1))
+                result = new("result_%d_%d_%d" % (g, h, piece), [P, width], F32)
+                nc.vector.scalar_tensor_tensor(
+                    result[:], z1[g, h][:, cols], slope[g, h][:], summed[g, h][:, cols], ALU.mult, ALU.add
+                )
+                nc.sync.dma_start(out=out[g, P * h : P * (h + 1), cols], in_=result[:])
 
         sum_squares(0, 0)
         sum_squares(1, 0)
-        make_gate(0, 0)
+        sum_squares(0, 1)
         inverse_roots(0)
-        make_gate(1, 0)
-        row_coefs(0, 0)
-        row_coefs(1, 0)
+        sum_squares(1, 1)
+        inverse_roots(1)
+        make_gate(0, 0)
         c0_product(0, 0)
+        z2_product(1, 0)
         c0_product(1, 0)
-        z1_product(1, 1)
         z2_product(0, 1)
+        make_gate(1, 0)
+        z2_product(1, 1)
+        row_coefs_on_vector(0)
+        row_coefs_on_scalar(1)
+        make_gate(0, 1)
+        make_gate(1, 1)
         first_term(0, 0)
         add_old(0, 0)
         first_term(1, 0)
-        c0_product(0, 1)
-        z2_product(1, 1)
-        c0_product(1, 1)
-        sum_squares(0, 1)
-        sum_squares(1, 1)
-        inverse_roots(1)
         add_old(1, 0)
-        make_gate(0, 1)
-        row_coefs(0, 1)
-        row_coefs(1, 1)
-        make_gate(1, 1)
+        c0_product(0, 1)
+        c0_product(1, 1)
         row_slope(0, 0)
         row_slope(1, 0)
         finish(0, 0)
         first_term(0, 1)
         add_old(0, 1)
-        finish(1, 0)
         first_term(1, 1)
         add_old(1, 1)
+        finish(1, 0)
         row_slope(0, 1)
         row_slope(1, 1)
         finish(0, 1)
-        finish(1, 1)
+        finish(1, 1, 2)

@@ -102,8 +102,11 @@ def tile_rows_brownorm_kernel(tc, x, w1_words, w1_scales, w2_words, w2_scales, g
         load_scales(nc.sync, w2_plane, w2_scales)
         w2 = load_words("w2", w2_words)
         wo = load_words("wo", wo_words)
-        old_sb = new("old_sb", [P, G * HALVES, N], F32)
-        nc.sync.dma_start(out=old_sb[:], in_=old.rearrange("g (h p) n -> p (g h) n", p=P))
+        old_sb = []
+        for h in range(HALVES):
+            old_half = new("old%d" % h, [P, G, N], F32)
+            nc.sync.dma_start(out=old_half[:], in_=old[:, P * h : P * (h + 1), :].rearrange("g p n -> p g n"))
+            old_sb.append(old_half)
 
         load_scales(nc.gpsimd, wo_plane, wo_scales)
 
@@ -125,10 +128,11 @@ def tile_rows_brownorm_kernel(tc, x, w1_words, w1_scales, w2_words, w2_scales, g
         def z2_product(g, h):
             product(z2[g], w2, w2_plane, x_codes, x_scales, g, h)
 
-        for h in range(HALVES):
-            for g in range(G):
-                z1_product(g, h)
+        z1_product(0, 0)
+        z1_product(1, 0)
         z2_product(0, 0)
+        z1_product(0, 1)
+        z1_product(1, 1)
 
         gain_cols = new("gain_cols", [P, P], F32)
         nc.vector.transpose(gain_cols[:], gain_rows[:])
@@ -188,7 +192,7 @@ def tile_rows_brownorm_kernel(tc, x, w1_words, w1_scales, w2_words, w2_scales, g
 
         def add_old(g, h):
             summed[g, h] = new("summed_%d_%d" % (g, h), [P, N], F32)
-            nc.gpsimd.tensor_tensor(summed[g, h][:], old_sb[:, HALVES * g + h, :], grad[g, h][:], ALU.subtract)
+            nc.gpsimd.tensor_tensor(summed[g, h][:], old_sb[h][:, g, :], grad[g, h][:], ALU.subtract)
 
         def row_slope(g, h):
             terms = new("terms_%d_%d" % (g, h), [P, N], F32)
@@ -209,11 +213,11 @@ def tile_rows_brownorm_kernel(tc, x, w1_words, w1_scales, w2_words, w2_scales, g
 
         sum_squares(0, 0)
         sum_squares(1, 0)
-        sum_squares(0, 1)
         inverse_roots(0)
+        make_gate(0, 0)
+        sum_squares(0, 1)
         sum_squares(1, 1)
         inverse_roots(1)
-        make_gate(0, 0)
         c0_product(0, 0)
         z2_product(1, 0)
         c0_product(1, 0)
@@ -226,11 +230,11 @@ def tile_rows_brownorm_kernel(tc, x, w1_words, w1_scales, w2_words, w2_scales, g
         make_gate(1, 1)
         first_term(0, 0)
         add_old(0, 0)
+        row_slope(0, 0)
         first_term(1, 0)
         add_old(1, 0)
         c0_product(0, 1)
         c0_product(1, 1)
-        row_slope(0, 0)
         row_slope(1, 0)
         finish(0, 0)
         first_term(0, 1)

import math
from contextlib import ExitStack

import concourse.mybir as mybir

G, D, M, N = 2, 256, 256, 512
FLOPS = 3 * 2 * G * D * M * N
EPS = 0.01

F32 = mybir.dt.float32
BF16 = mybir.dt.bfloat16
I32 = mybir.dt.int32
U32 = mybir.dt.uint32
U8 = mybir.dt.uint8
FP8X4 = mybir.dt.float8_e4m3fn_x4
FP4X4 = mybir.dt.float4_e2m1fn_x4
ALU = mybir.AluOpType
ACT = mybir.ActivationFunctionType

P = 128
PACK = 4
ROWS = D // PACK
QUAD = 32
HALVES = M // P
HALF_N = N // 2
X_VECTOR_COLS = 64


def tile_rows_brownorm_kernel(tc, x, w1_words, w1_scales, w2_words, w2_scales, gn, wo_words, wo_scales, dy, old, out):
    nc = tc.nc
    with ExitStack() as ctx:
        sb = ctx.enter_context(tc.tile_pool(name="sb", bufs=1))
        ps = ctx.enter_context(tc.psum_pool(name="ps", bufs=1))
        ctx.enter_context(tc.manual_schedule())

        def new(name, shape, dtype):
            return sb.tile(shape, dtype, name=name, align_bytes=64)

        def load_rows(name, src):
            raw = new(name, [P, PACK, N], F32)
            nc.sync.dma_start(out=raw[:], in_=src.rearrange("g (p j) n -> (g p) j n", j=PACK))
            return raw

        def load_words(name, src):
            words = new(name, [P, 2 * M], U8)
            nc.sync.dma_start(out=words[:].bitcast(I32), in_=src.rearrange("g p b -> (g p) b").bitcast(I32))
            return words

        def zeroed_plane(name):
            plane = new(name, [P, M], U8)
            nc.vector.memset(plane[:].bitcast(I32), 0)
            return plane

        def load_scales(queue, plane, src):
            rows = src.rearrange("g t m -> (g t) m").bitcast(I32)
            for q in range(P // QUAD):
                queue.dma_start(out=plane[QUAD * q : QUAD * q + 4, :].bitcast(I32), in_=rows[4 * q : 4 * q + 4, :])

        def interleave(copy, dst, raw, half, lo, hi):
            cols = slice(half * HALF_N + lo, half * HALF_N + hi)
            copy(
                out=dst[:, lo:hi, :].rearrange("p (c i) j -> p c j i", i=4),
                in_=raw[:, :, cols].rearrange("p j (c i) -> p c j i", i=4),
            )

        def quantize(codes, scales, grouped, half):
            cols = slice(half * HALF_N, (half + 1) * HALF_N)
            nc.vector.quantize_mx(
                out=codes[:, cols].bitcast(FP8X4), scales=scales[:, cols], in_=grouped[:].rearrange("p c j -> p (c j)")
            )

        def product(bank, words, plane, codes, scales, g, h):
            rows = slice(ROWS * g, ROWS * (g + 1))
            nc.tensor.matmul_mx(
                out=bank[:],
                lhsT=words[rows, 2 * P * h : 2 * P * (h + 1)].bitcast(FP4X4),
                lhsT_scale=plane[rows, P * h : P * (h + 1)],
                rhs=codes[rows, :].bitcast(FP8X4),
                rhs_scale=scales[rows, :],
                start=True,
                stop=True,
            )

        w1_plane = zeroed_plane("w1_plane")
        wo_plane = zeroed_plane("wo_plane")
        gain_rows = new("gain_rows", [P, P], F32)
        nc.vector.memset(gain_rows[:], 0.0)
        w2_plane = zeroed_plane("w2_plane")
        minus_half = new("minus_half", [P, G], F32)
        nc.vector.memset(minus_half[:], -0.5)
        warm = new("warm", [P, G], F32)
        nc.scalar.activation(warm[:], minus_half[:], ACT.Sigmoid)

        x_raw = load_rows("x_raw", x)
        load_scales(nc.sync, w1_plane, w1_scales)
        w1 = load_words("w1", w1_words)
        nc.sync.dma_start(
            out=gain_rows[0:P:QUAD, :].rearrange("q (c i) -> q c i", i=QUAD),
            in_=gn.rearrange("g m o -> (g m o)").rearrange("(c q i) -> q c i", q=P // QUAD, i=QUAD),
        )
        dy_raw = load_rows("dy_raw", dy)
        load_scales(nc.sync, w2_plane, w2_scales)
        w2 = load_words("w2", w2_words)
        wo = load_words("wo", wo_words)
        old_sb = []
        for h in range(HALVES):
            old_half = new("old%d" % h, [P, G, N], F32)
            nc.sync.dma_start(out=old_half[:], in_=old[:, P * h : P * (h + 1), :].rearrange("g p n -> p g n"))
            old_sb.append(old_half)

        load_scales(nc.gpsimd, wo_plane, wo_scales)

        x_codes, x_scales = new("x_codes", [P, N], U32), new("x_scales", [P, N], U8)
        x_lo, x_hi = new("x_lo", [P, HALF_N, PACK], BF16), new("x_hi", [P, HALF_N, PACK], BF16)
        interleave(nc.vector.tensor_copy, x_lo, x_raw, 0, 0, HALF_N)
        interleave(nc.scalar.copy, x_hi, x_raw, 1, X_VECTOR_COLS, HALF_N)
        interleave(nc.vector.tensor_copy, x_hi, x_raw, 1, 0, X_VECTOR_COLS)
        quantize(x_codes, x_scales, x_lo, 0)
        quantize(x_codes, x_scales, x_hi, 1)

        z1 = {(g, h): ps.tile([P, N], F32, name="z1_%d_%d" % (g, h)) for g in range(G) for h in range(HALVES)}
        z2 = [ps.tile([P, N], F32, name="z2_%d" % g) for g in range(G)]
        c0 = [ps.tile([P, N], F32, name="c0_%d" % g) for g in range(G)]

        def z1_product(g, h):
            product(z1[g, h], w1, w1_plane, x_codes, x_scales, g, h)

        def z2_product(g, h):
            product(z2[g], w2, w2_plane, x_codes, x_scales, g, h)

        z1_product(0, 0)
        z1_product(1, 0)
        z2_product(0, 0)
        z1_product(0, 1)
        z1_product(1, 1)

        gain_cols = new("gain_cols", [P, P], F32)
        nc.vector.transpose(gain_cols[:], gain_rows[:])
        factors = new("factors", [P, 2, 8], F32)
        nc.vector.tensor_scalar(
            factors[:, 0, 0 : HALVES * G].rearrange("p (h g) -> p h g", g=G),
            gain_cols[:].rearrange("p (g h i) -> p h g i", g=G, h=HALVES)[:, :, :, 0],
            -math.sqrt(N),
            None,
            ALU.mult,
        )

        dy_codes, dy_scales = new("dy_codes", [P, N], U32), new("dy_scales", [P, N], U8)
        dy_halves = [new("dy_half%d" % half, [P, HALF_N, PACK], BF16) for half in range(2)]
        for half in range(2):
            interleave(nc.vector.tensor_copy, dy_halves[half], dy_raw, half, 0, HALF_N)
        for half in range(2):
            quantize(dy_codes, dy_scales, dy_halves[half], half)

        def c0_product(g, h):
            product(c0[g], wo, wo_plane, dy_codes, dy_scales, g, h)

        square_sums, coefs, gate, grad, slope, summed = {}, {}, {}, {}, {}, {}

        for h in range(HALVES):
            square_sums[h] = new("square_sums%d" % h, [P, G], F32)

        def sum_squares(g, h):
            squares = new("squares_%d_%d" % (g, h), [P, N], BF16)
            nc.scalar.activation(squares[:], z1[g, h][:], ACT.Square, accum_out=square_sums[h][:, g : g + 1])

        def inverse_roots(h):
            total = new("total%d" % h, [P, G], F32)
            nc.scalar.activation(total[:], square_sums[h][:], ACT.Copy, bias=N * EPS)
            nc.gpsimd.tensor_tensor(factors[:, 1, G * h : G * (h + 1)], total[:], minus_half[:], ALU.pow)

        def row_coefs_on_vector(h):
            cols = slice(G * h, G * (h + 1))
            coefs[h] = new("coefs%d" % h, [P, 2, G], F32)
            nc.vector.tensor_tensor(coefs[h][:], factors[:, :, cols], factors[:, 1:2, cols].to_broadcast([P, 2, G]), ALU.mult)

        def row_coefs_on_scalar(h):
            coefs[h] = new("coefs%d" % h, [P, 2, G], F32)
            for g in range(G):
                col = G * h + g
                nc.scalar.activation(coefs[h][:, :, g], factors[:, :, col], ACT.Copy, scale=factors[:, 1, col : col + 1])

        def make_gate(g, h):
            gate[g, h] = new("gate_%d_%d" % (g, h), [P, N], F32)
            nc.scalar.activation(gate[g, h][:], z2[g][:], ACT.Sigmoid)

        def first_term(g, h):
            grad[g, h] = new("grad_%d_%d" % (g, h), [P, N], F32)
            nc.vector.scalar_tensor_tensor(
                grad[g, h][:], c0[g][:], coefs[h][:, 0, g : g + 1], gate[g, h][:], ALU.mult, ALU.mult
            )

        def add_old(g, h):
            summed[g, h] = new("summed_%d_%d" % (g, h), [P, N], F32)
            nc.gpsimd.tensor_tensor(summed[g, h][:], old_sb[h][:, g, :], grad[g, h][:], ALU.subtract)

        def row_slope(g, h):
            terms = new("terms_%d_%d" % (g, h), [P, N], F32)
            slope[g, h] = new("slope_%d_%d" % (g, h), [P, 1], F32)
            nc.vector.scalar_tensor_tensor(
                terms[:], z1[g, h][:], coefs[h][:, 1, g : g + 1], grad[g, h][:], ALU.mult, ALU.mult, accum_out=slope[g, h][:]
            )

        def finish(g, h, pieces=1):
            width = N // pieces
            for piece in range(pieces):
                cols = slice(width * piece, width * (piece + 1))
                result = new("result_%d_%d_%d" % (g, h, piece), [P, width], F32)
                nc.vector.scalar_tensor_tensor(
                    result[:], z1[g, h][:, cols], slope[g, h][:], summed[g, h][:, cols], ALU.mult, ALU.add
                )
                nc.sync.dma_start(out=out[g, P * h : P * (h + 1), cols], in_=result[:])

        sum_squares(0, 0)
        sum_squares(1, 0)
        inverse_roots(0)
        make_gate(0, 0)
        sum_squares(0, 1)
        sum_squares(1, 1)
        inverse_roots(1)
        c0_product(0, 0)
        z2_product(1, 0)
        c0_product(1, 0)
        z2_product(0, 1)
        make_gate(1, 0)
        z2_product(1, 1)
        row_coefs_on_vector(0)
        row_coefs_on_scalar(1)
        make_gate(0, 1)
        make_gate(1, 1)
        first_term(0, 0)
        add_old(0, 0)
        row_slope(0, 0)
        first_term(1, 0)
        add_old(1, 0)
        c0_product(0, 1)
        c0_product(1, 1)
        row_slope(1, 0)
        finish(0, 0)
        first_term(0, 1)
        add_old(0, 1)
        first_term(1, 1)
        add_old(1, 1)
        finish(1, 0)
        row_slope(0, 1)
        row_slope(1, 1)
        finish(0, 1)
        finish(1, 1, 2)
